import numpy as np
import ml_dtypes


def mxq(x, axis, fmt="e4m3"):
    dtype, down = {"e4m3": (ml_dtypes.float8_e4m3fn, 7), "e5m2": (ml_dtypes.float8_e5m2, 14)}[fmt]
    v = np.moveaxis(np.asarray(x, np.float32).astype(ml_dtypes.bfloat16).astype(np.float64), axis, -1)
    blocks = v.reshape(v.shape[:-1] + (-1, 32))
    amax = np.abs(blocks).max(-1, keepdims=True)
    byte = np.maximum(np.where(amax > 0, np.frexp(amax)[1] - 1 + 127, 0) - down, 1)
    scale = np.exp2(byte - 127.0)
    codes = (blocks / scale).astype(np.float32).astype(dtype).astype(np.float64)
    return np.moveaxis((codes * scale).reshape(v.shape), -1, axis)


WIDE = False


def mx_kscale(k):
    if not WIDE:
        return np.ones(k)
    levels = np.array([10, -10, 5, -5, 0])
    if k % 512:
        return np.exp2(np.random.permutation(np.resize(levels, k // 32))).repeat(32)
    a = np.empty((k // 512, 16))
    for p in range(k // 512):
        a[p, :8] = np.random.permutation(np.resize(levels, 8))
        for g in range(8):
            far = levels[np.abs(levels - a[p, g]) >= 10]
            a[p, g + 8] = far[np.random.randint(len(far))]
    return np.exp2(a.ravel()).repeat(32)


def f64(x):
    return np.asarray(x).astype(np.float64)


def striped(idx):
    return np.tile(idx.reshape(-1, 16).T, (8, 1)).astype(np.uint16)


def unstriped(offs):
    return offs[:16].T.reshape(-1).astype(np.int64)


def pack_weight(w):
    k, n = w.shape
    w = f64(np.asarray(w, np.float32).astype(ml_dtypes.bfloat16)).reshape(k // 32, 32, n)
    amax = np.abs(w).max(1)
    byte = np.clip(np.where(amax > 0, np.frexp(amax)[1] - 1 + 127 - 7, 1), 1, 254)
    scaled = (w * np.exp2(127.0 - byte)[:, None, :]).reshape(k, n).astype(np.float32)
    words = np.ascontiguousarray(scaled.reshape(k // 512, 128, 4, n).transpose(0, 1, 3, 2)).astype(ml_dtypes.float8_e4m3fn).view(np.uint8)
    return words, np.ascontiguousarray(byte.astype(np.uint8).reshape(k // 512, 16, n))


def unpack_weight(words, scales):
    g, p, n, _ = words.shape
    vals = np.ascontiguousarray(words).view(ml_dtypes.float8_e4m3fn).astype(np.float64) * np.repeat(np.exp2(scales.astype(np.float64) - 127.0), 8, axis=1)[..., None]
    return vals.transpose(0, 1, 3, 2).reshape(g * 512, n)


def sigmoid(v):
    return 1.0 / (1.0 + np.exp(-np.maximum(v, -700.0)))


K, T, S, N, G, H, U = 512, 2048, 256, 512, 2048, 512, 1024


def setup_inputs():
    n = np.random.standard_normal
    s = mx_kscale(K)[:, None]
    u = mx_kscale(K)
    packed_xT = pack_weight(n((K, T)) * s)
    packed_dT = pack_weight(n((K, G)) / s)
    return {
        "x_words": packed_xT[0],
        "x_scales": packed_xT[1],
        "d_words": packed_dT[0],
        "d_scales": packed_dT[1],
        "sl": np.random.uniform(1.0, 2.0, (H, 1)).astype(np.float32),
        "th": (0.5 * n((H, 1))).astype(np.float32),
        "gn": (np.random.uniform(0.5, 1.5, (H, 1)) * u[:, None]).astype(np.float32),
        "w1": (n((H, N)) / np.sqrt(H) / u[:, None]).astype(np.float32),
        "mem": n((N, U)).astype(np.float32),
        "offs": striped(np.random.permutation(T)[:S]),
        "ci": striped(np.random.permutation(G)[:H]),
        "n1": striped(np.random.permutation(S)),
        "n2": striped(np.random.permutation(S)),
        "n3": striped(np.random.permutation(U)[:S]),
    }


def reference(x_words, x_scales, d_words, d_scales, sl, th, gn, w1, mem, offs, ci, n1, n2, n3):
    old = f64(mem)[:, unstriped(n3)]
    d_ci = unpack_weight(d_words, d_scales)[:, unstriped(ci)]
    xq = unpack_weight(x_words, x_scales)[:, unstriped(offs)]
    s = 0.0625 * (d_ci.T @ xq)
    st = s - s[:, unstriped(n1)]
    sg = sigmoid(f64(sl) * (st[:, unstriped(n2)] - f64(th)))
    z = f64(gn) * (s * sg)
    h = mxq(f64(w1), 0, "e4m3").T @ mxq(z, 0, "e4m3")
    nw = old + sigmoid(h) * (h - old)
    out = f64(mem).copy()
    out[:, unstriped(n3)] = nw
    return out

@@ -1,0 +1,177 @@
+from contextlib import ExitStack
+
+import concourse.mybir as mybir
+
+K, T, S, N, G, H, U = 512, 2048, 256, 512, 2048, 512, 1024
+FLOPS = 2 * K * H * S + 2 * H * N * S
+
+F32 = mybir.dt.float32
+BF16 = mybir.dt.bfloat16
+I32 = mybir.dt.int32
+U32 = mybir.dt.uint32
+U16 = mybir.dt.uint16
+U8 = mybir.dt.uint8
+FP8X4 = mybir.dt.float8_e4m3fn_x4
+ACT = mybir.ActivationFunctionType
+ALU = mybir.AluOpType
+
+P = 128
+PACK = 4
+QUADS = 4
+QUAD = 32
+SPARE = 16
+ALIGN = 64
+
+
+def interleave(nc, dst, src):
+    nc.vector.tensor_copy(
+        out=dst.rearrange("p (c i) t -> p c t i", i=4),
+        in_=src.rearrange("p t (c i) -> p c t i", i=4),
+    )
+
+
+def tile_picked_dwlehqpaget_none_p_kernel(
+    tc, x_words, x_scales, d_words, d_scales, sl, th, gn, w1, mem, offs, ci, n1, n2, n3, out
+):
+    nc = tc.nc
+    with ExitStack() as ctx:
+        lists = ctx.enter_context(tc.tile_pool(name="lists", bufs=1))
+        sb = ctx.enter_context(tc.tile_pool(name="sb", bufs=1))
+        psum = ctx.enter_context(tc.psum_pool(name="psum", bufs=1))
+
+        ci_t = lists.tile([P, H // 16], U16, name="ci_t")
+        offs_t = lists.tile([P, S // 16], U16, name="offs_t")
+        n1_t = lists.tile([P, S // 16], U16, name="n1_t")
+        n2_t = lists.tile([P, S // 16], U16, name="n2_t")
+        n3_t = lists.tile([P, S // 16], U16, name="n3_t")
+
+        d_table = sb.tile([P, G], U32, name="d_table", tag="d_table", align_bytes=ALIGN)
+        x_table = sb.tile([P, T], U32, name="x_table", tag="x_table", align_bytes=ALIGN)
+        d_bytes = sb.tile([P, G], U8, name="d_bytes", tag="d_bytes", align_bytes=ALIGN)
+        x_bytes = sb.tile([P, T], U8, name="x_bytes", tag="x_bytes", align_bytes=ALIGN)
+
+        w_raw = sb.tile([P, PACK, N], F32, name="w_raw")
+        page = [sb.tile([P, U], F32, name=f"page{u}") for u in range(N // P)]
+        rows = sb.tile([P, 3, 8], F32, name="rows")
+
+        nc.vector.memset(d_bytes[:].bitcast(I32), 0)
+        nc.vector.memset(x_bytes[:].bitcast(I32), 0)
+        nc.sync.dma_start(ci_t[:], ci)
+        nc.sync.dma_start(offs_t[:], offs)
+        nc.sync.dma_start(n1_t[:], n1)
+        nc.sync.dma_start(d_table[:].bitcast(I32), d_words[0].rearrange("p n t -> p (n t)").bitcast(I32))
+        nc.sync.dma_start(x_table[:].bitcast(I32), x_words[0].rearrange("p n t -> p (n t)").bitcast(I32))
+        nc.sync.dma_start(w_raw[:], w1.rearrange("(p t) m -> p t m", t=PACK))
+        nc.sync.dma_start(n2_t[:], n2)
+        nc.sync.dma_start(n3_t[:], n3)
+        for u in range(N // P):
+            nc.sync.dma_start(page[u][:], mem[P * u : P * (u + 1), :])
+        for table, scales in ((d_bytes, d_scales), (x_bytes, x_scales)):
+            for q in range(QUADS):
+                nc.scalar.dma_start(
+                    table[QUAD * q : QUAD * q + 4, :].bitcast(I32), scales[0, 4 * q : 4 * q + 4, :].bitcast(I32)
+                )
+        for a, vec in enumerate((sl, th, gn)):
+            nc.scalar.dma_start(rows[:, a, :PACK], vec.rearrange("(p t) o -> p (t o)", t=PACK))
+        slope, thresh, gain = rows[:, 0, :PACK], rows[:, 1, :PACK], rows[:, 2, :PACK]
+        bias = sb.tile([P, PACK], F32, name="bias")
+        scores = [sb.tile([P, S + SPARE], F32, name=f"scores{t}") for t in range(PACK)]
+        for t in range(PACK):
+            nc.vector.memset(scores[t][:, S:], 0.0)
+
+        d_codes = sb.tile([P, H], U32, name="d_codes", tag="d_codes", align_bytes=ALIGN)
+        d_plane = sb.tile([P, H], U8, name="d_plane", align_bytes=ALIGN)
+        x_codes = sb.tile([P, S], U32, name="x_codes", tag="x_codes", align_bytes=ALIGN)
+        x_plane = sb.tile([P, S], U8, name="x_plane", align_bytes=ALIGN)
+        nc.vector.tensor_copy(d_plane[:].rearrange("p (t m) -> p m t", t=PACK), d_bytes[:].indirect(ci_t[:]))
+        nc.vector.tensor_copy(d_codes[:].rearrange("p (t m) -> p m t", t=PACK), d_table[:].indirect(ci_t[:]))
+        nc.vector.tensor_copy(x_plane[:], x_bytes[:].indirect(offs_t[:]))
+        nc.vector.tensor_copy(x_codes[:], x_table[:].indirect(offs_t[:]))
+
+        s_acc = [psum.tile([P, S], F32, name=f"s_acc{t}") for t in range(PACK)]
+        for t in range(PACK):
+            cols = slice(P * t, P * (t + 1))
+            nc.tensor.matmul_mx(
+                out=s_acc[t][:],
+                lhsT=d_codes[:, cols].bitcast(FP8X4),
+                lhsT_scale=d_plane[:, cols],
+                rhs=x_codes[:].bitcast(FP8X4),
+                rhs_scale=x_plane[:],
+                start=True,
+                stop=True,
+            )
+
+        w_codes = [sb.tile([P, P], U32, name=f"w_codes{u}", align_bytes=ALIGN) for u in range(N // P)]
+        w_plane = [sb.tile([P, P], U8, name=f"w_plane{u}", align_bytes=ALIGN) for u in range(N // P)]
+        w_bf = [sb.tile([P, P, PACK], BF16, name=f"w_bf{u}", align_bytes=ALIGN) for u in range(N // P)]
+
+        def quantize(codes, plane, grouped):
+            nc.vector.quantize_mx(
+                out=codes[:].bitcast(FP8X4), scales=plane[:], in_=grouped[:].rearrange("p c t -> p (c t)")
+            )
+
+        nc.vector.scalar_tensor_tensor(bias[:], slope, -1.0, thresh, ALU.mult, ALU.mult)
+        for t in range(PACK):
+            nc.vector.tensor_scalar(scores[t][:, :S], s_acc[t][:], 0.0625, None, ALU.mult)
+        diff = [sb.tile([P, 2 * S], F32, name=f"diff{t}", tag=f"diff{t}") for t in range(PACK)]
+        for t in range(PACK):
+            nc.scalar.activation(diff[t][:, S:], scores[t][:].indirect(n1_t[:]), ACT.Copy)
+            nc.vector.tensor_tensor(diff[t][:, :S], scores[t][:, :S], diff[t][:, S:], ALU.subtract)
+            if t > 0:
+                interleave(nc, w_bf[t - 1][:], w_raw[:, :, P * (t - 1) : P * t])
+
+        z = sb.tile([P, PACK, S], F32, name="z")
+        for t in range(PACK):
+            gate = sb.tile([P, S], F32, name=f"gate{t}")
+            nc.scalar.activation(
+                gate[:],
+                diff[t][:].indirect(n2_t[:]),
+                ACT.Sigmoid,
+                bias=bias[:, t : t + 1],
+                scale=slope[:, t : t + 1],
+            )
+            nc.vector.scalar_tensor_tensor(
+                z[:, t, :], scores[t][:, :S], gain[:, t : t + 1], gate[:], ALU.mult, ALU.mult
+            )
+            if t == 0:
+                interleave(nc, w_bf[3][:], w_raw[:, :, P * 3 : P * 4])
+            if t == 1:
+                quantize(w_codes[0], w_plane[0], w_bf[0])
+        z_bf = sb.tile([P, S, PACK], BF16, name="z_bf", align_bytes=ALIGN)
+        z_codes = sb.tile([P, S], U32, name="z_codes", align_bytes=ALIGN)
+        z_plane = sb.tile([P, S], U8, name="z_plane", align_bytes=ALIGN)
+        interleave(nc, z_bf[:], z[:])
+        quantize(w_codes[1], w_plane[1], w_bf[1])
+        quantize(z_codes, z_plane, z_bf)
+        quantize(w_codes[2], w_plane[2], w_bf[2])
+        quantize(w_codes[3], w_plane[3], w_bf[3])
+
+        olds = sb.tile([P, N // P, S], F32, name="olds", tag=f"diff{PACK - 1}")
+        old = [olds[:, u, :] for u in range(N // P)]
+        for u in range(N // P):
+            nc.scalar.activation(old[u], page[u][:].indirect(n3_t[:]), ACT.Copy)
+
+        new = []
+        for u in range(N // P):
+            h_acc = psum.tile([P, S], F32, name=f"h_acc{u}")
+            nc.tensor.matmul_mx(
+                out=h_acc[:],
+                lhsT=w_codes[u][:].bitcast(FP8X4),
+                lhsT_scale=w_plane[u][:],
+                rhs=z_codes[:].bitcast(FP8X4),
+                rhs_scale=z_plane[:],
+                start=True,
+                stop=True,
+            )
+            mix = sb.tile([P, S], F32, name=f"mix{u}")
+            nc.scalar.activation(mix[:], h_acc[:], ACT.Sigmoid)
+            step = sb.tile([P, S], F32, name=f"step{u}")
+            nc.vector.tensor_tensor(step[:], h_acc[:], old[u], ALU.subtract)
+            moved = sb.tile([P, S], F32, name=f"moved{u}")
+            nc.vector.tensor_tensor(moved[:], step[:], mix[:], ALU.mult)
+            fresh = sb.tile([P, S], F32, name=f"fresh{u}")
+            nc.vector.tensor_tensor(fresh[:], moved[:], old[u], ALU.add)
+            new.append(fresh)
+        for u in range(N // P):
+            nc.scalar.activation(page[u][:].indirect(n3_t[:]), new[u][:], ACT.Copy)
+            nc.sync.dma_start(out[P * u : P * (u + 1), :], page[u][:])

@@ -21,6 +21,7 @@ QUADS = 4
 QUAD = 32
 SPARE = 16
 ALIGN = 64
+HEAD = 512
 
 
 def interleave(nc, dst, src):
@@ -50,45 +51,55 @@ def tile_picked_dwlehqpaget_none_p_kernel(
         d_bytes = sb.tile([P, G], U8, name="d_bytes", tag="d_bytes", align_bytes=ALIGN)
         x_bytes = sb.tile([P, T], U8, name="x_bytes", tag="x_bytes", align_bytes=ALIGN)
 
-        w_raw = sb.tile([P, PACK, N], F32, name="w_raw")
-        page = [sb.tile([P, U], F32, name=f"page{u}") for u in range(N // P)]
         rows = sb.tile([P, 3, 8], F32, name="rows")
+
+        picked_bytes = sb.tile([P, H + S], U8, name="picked_bytes", align_bytes=ALIGN)
+        planes = sb.tile([P, H + S], U8, name="planes", align_bytes=ALIGN)
+        d_codes = sb.tile([P, H], U32, name="d_codes", tag="d_codes", align_bytes=ALIGN)
+        x_codes = sb.tile([P, S], U32, name="x_codes", tag="x_codes", align_bytes=ALIGN)
+        scores = [sb.tile([P, S + SPARE], F32, name=f"scores{t}") for t in range(PACK)]
 
         nc.vector.memset(d_bytes[:].bitcast(I32), 0)
         nc.vector.memset(x_bytes[:].bitcast(I32), 0)
-        nc.sync.dma_start(ci_t[:], ci)
-        nc.sync.dma_start(offs_t[:], offs)
-        nc.sync.dma_start(n1_t[:], n1)
-        nc.sync.dma_start(d_table[:].bitcast(I32), d_words[0].rearrange("p n t -> p (n t)").bitcast(I32))
-        nc.sync.dma_start(x_table[:].bitcast(I32), x_words[0].rearrange("p n t -> p (n t)").bitcast(I32))
-        nc.sync.dma_start(w_raw[:], w1.rearrange("(p t) m -> p t m", t=PACK))
-        nc.sync.dma_start(n2_t[:], n2)
-        nc.sync.dma_start(n3_t[:], n3)
-        for u in range(N // P):
-            nc.sync.dma_start(page[u][:], mem[P * u : P * (u + 1), :])
-        for table, scales in ((d_bytes, d_scales), (x_bytes, x_scales)):
-            for q in range(QUADS):
-                nc.scalar.dma_start(
-                    table[QUAD * q : QUAD * q + 4, :].bitcast(I32), scales[0, 4 * q : 4 * q + 4, :].bitcast(I32)
-                )
-        for a, vec in enumerate((sl, th, gn)):
-            nc.scalar.dma_start(rows[:, a, :PACK], vec.rearrange("(p t) o -> p (t o)", t=PACK))
-        slope, thresh, gain = rows[:, 0, :PACK], rows[:, 1, :PACK], rows[:, 2, :PACK]
-        bias = sb.tile([P, PACK], F32, name="bias")
-        scores = [sb.tile([P, S + SPARE], F32, name=f"scores{t}") for t in range(PACK)]
+        warm = sb.tile([P, 16], F32, name="warm")
+        nc.vector.memset(warm[:, :1], 0.0)
+        nc.scalar.activation(warm[:, 8:9], warm[:, :1], ACT.Sigmoid)
+        nc.vector.memset(planes[:].bitcast(I32), 0)
         for t in range(PACK):
             nc.vector.memset(scores[t][:, S:], 0.0)
+        d_src = d_words[0].rearrange("p n t -> p (n t)").bitcast(I32)
+        nc.sync.dma_start(d_table[:, :HEAD].bitcast(I32), d_src[:, :HEAD])
+        nc.sync.dma_start(ci_t[:], ci)
+        nc.sync.dma_start(d_bytes[0:P:8, :].bitcast(I32), d_scales[0].bitcast(I32))
+        nc.sync.dma_start(offs_t[:], offs)
+        nc.sync.dma_start(x_bytes[0:P:8, :].bitcast(I32), x_scales[0].bitcast(I32))
+        nc.sync.dma_start(d_table[:, HEAD:].bitcast(I32), d_src[:, HEAD:])
+        nc.sync.dma_start(n1_t[:], n1)
+        nc.sync.dma_start(x_table[:].bitcast(I32), x_words[0].rearrange("p n t -> p (n t)").bitcast(I32))
+        nc.sync.dma_start(n2_t[:], n2)
+        nc.sync.dma_start(n3_t[:], n3)
 
-        d_codes = sb.tile([P, H], U32, name="d_codes", tag="d_codes", align_bytes=ALIGN)
-        d_plane = sb.tile([P, H], U8, name="d_plane", align_bytes=ALIGN)
-        x_codes = sb.tile([P, S], U32, name="x_codes", tag="x_codes", align_bytes=ALIGN)
-        x_plane = sb.tile([P, S], U8, name="x_plane", align_bytes=ALIGN)
-        nc.vector.tensor_copy(d_plane[:].rearrange("p (t m) -> p m t", t=PACK), d_bytes[:].indirect(ci_t[:]))
+        nc.vector.tensor_copy(picked_bytes[:, :H].rearrange("p (t m) -> p m t", t=PACK), d_bytes[:].indirect(ci_t[:]))
+        nc.vector.tensor_copy(picked_bytes[:, H:], x_bytes[:].indirect(offs_t[:]))
+        for q in range(QUADS):
+            nc.sync.dma_start(
+                planes[QUAD * q : QUAD * q + 4, :].bitcast(I32), picked_bytes[QUAD * q : QUAD * (q + 1) : 8, :].bitcast(I32)
+            )
+        d_plane, x_plane = planes[:, :H], planes[:, H:]
         nc.vector.tensor_copy(d_codes[:].rearrange("p (t m) -> p m t", t=PACK), d_table[:].indirect(ci_t[:]))
-        nc.vector.tensor_copy(x_plane[:], x_bytes[:].indirect(offs_t[:]))
         nc.vector.tensor_copy(x_codes[:], x_table[:].indirect(offs_t[:]))
 
-        s_acc = [psum.tile([P, S], F32, name=f"s_acc{t}") for t in range(PACK)]
+        w_raw = sb.tile([P, PACK, N], F32, name="w_raw", tag="x_bytes", align_bytes=ALIGN)
+        nc.sync.dma_start(w_raw[:], w1.rearrange("(p t) m -> p t m", t=PACK))
+        for a, vec in enumerate((sl, th, gn)):
+            nc.gpsimd.dma_start(rows[:, a, :PACK], vec.rearrange("(p t) o -> p (t o)", t=PACK))
+        slope, thresh, gain = rows[:, 0, :PACK], rows[:, 1, :PACK], rows[:, 2, :PACK]
+        bias = sb.tile([P, PACK], F32, name="bias")
+        slope_thresh = sb.tile([P, PACK], F32, name="slope_thresh")
+        nc.gpsimd.tensor_tensor(slope_thresh[:], slope, thresh, ALU.mult)
+        nc.gpsimd.tensor_scalar(bias[:], slope_thresh[:], -1.0, None, ALU.mult)
+
+        s_acc = [psum.tile([P, S], F32, name=f"s_acc{t}", tag=f"s_acc{t}") for t in range(PACK)]
         for t in range(PACK):
             cols = slice(P * t, P * (t + 1))
             nc.tensor.matmul_mx(
@@ -96,31 +107,40 @@ def tile_picked_dwlehqpaget_none_p_kernel(
                 lhsT=d_codes[:, cols].bitcast(FP8X4),
                 lhsT_scale=d_plane[:, cols],
                 rhs=x_codes[:].bitcast(FP8X4),
-                rhs_scale=x_plane[:],
+                rhs_scale=x_plane,
                 start=True,
                 stop=True,
             )
 
+        page_tags = ("d_table", "x_table", "d_codes", "x_codes")
+        page = [sb.tile([P, U], F32, name=f"page{u}", tag=page_tags[u], align_bytes=ALIGN) for u in range(N // P)]
+        for u in range(N // P):
+            nc.sync.dma_start(page[u][:], mem[P * u : P * (u + 1), :])
+
         w_codes = [sb.tile([P, P], U32, name=f"w_codes{u}", align_bytes=ALIGN) for u in range(N // P)]
         w_plane = [sb.tile([P, P], U8, name=f"w_plane{u}", align_bytes=ALIGN) for u in range(N // P)]
-        w_bf = [sb.tile([P, P, PACK], BF16, name=f"w_bf{u}", align_bytes=ALIGN) for u in range(N // P)]
 
         def quantize(codes, plane, grouped):
             nc.vector.quantize_mx(
                 out=codes[:].bitcast(FP8X4), scales=plane[:], in_=grouped[:].rearrange("p c t -> p (c t)")
             )
 
-        nc.vector.scalar_tensor_tensor(bias[:], slope, -1.0, thresh, ALU.mult, ALU.mult)
+        def round_weights(u, tag):
+            grouped = sb.tile([P, P, PACK], BF16, name=f"w_bf{u}", tag=tag, align_bytes=ALIGN)
+            interleave(nc, grouped[:], w_raw[:, :, P * u : P * (u + 1)])
+            return grouped
+
         for t in range(PACK):
             nc.vector.tensor_scalar(scores[t][:, :S], s_acc[t][:], 0.0625, None, ALU.mult)
         diff = [sb.tile([P, 2 * S], F32, name=f"diff{t}", tag=f"diff{t}") for t in range(PACK)]
+        w_bf = {}
         for t in range(PACK):
             nc.scalar.activation(diff[t][:, S:], scores[t][:].indirect(n1_t[:]), ACT.Copy)
             nc.vector.tensor_tensor(diff[t][:, :S], scores[t][:, :S], diff[t][:, S:], ALU.subtract)
-            if t > 0:
-                interleave(nc, w_bf[t - 1][:], w_raw[:, :, P * (t - 1) : P * t])
+            if t % 2 == 1:
+                w_bf[t // 2] = round_weights(t // 2, f"w_bf{t // 2}")
 
-        z = sb.tile([P, PACK, S], F32, name="z")
+        z = sb.tile([P, PACK, S], F32, name="z", tag="z", align_bytes=ALIGN)
         for t in range(PACK):
             gate = sb.tile([P, S], F32, name=f"gate{t}")
             nc.scalar.activation(
@@ -133,45 +153,75 @@ def tile_picked_dwlehqpaget_none_p_kernel(
             nc.vector.scalar_tensor_tensor(
                 z[:, t, :], scores[t][:, :S], gain[:, t : t + 1], gate[:], ALU.mult, ALU.mult
             )
-            if t == 0:
-                interleave(nc, w_bf[3][:], w_raw[:, :, P * 3 : P * 4])
-            if t == 1:
-                quantize(w_codes[0], w_plane[0], w_bf[0])
-        z_bf = sb.tile([P, S, PACK], BF16, name="z_bf", align_bytes=ALIGN)
-        z_codes = sb.tile([P, S], U32, name="z_codes", align_bytes=ALIGN)
-        z_plane = sb.tile([P, S], U8, name="z_plane", align_bytes=ALIGN)
-        interleave(nc, z_bf[:], z[:])
-        quantize(w_codes[1], w_plane[1], w_bf[1])
-        quantize(z_codes, z_plane, z_bf)
-        quantize(w_codes[2], w_plane[2], w_bf[2])
-        quantize(w_codes[3], w_plane[3], w_bf[3])
+            if t < 2:
+                quantize(w_codes[t], w_plane[t], w_bf[t])
+        halves = [slice(0, S // 2), slice(S // 2, S)]
+        z_bf = [sb.tile([P, S // 2, PACK], BF16, name=f"z_bf{a}", tag=f"z_bf{a}", align_bytes=ALIGN) for a in range(2)]
+        z_codes = [sb.tile([P, S // 2], U32, name=f"z_codes{a}", align_bytes=ALIGN) for a in range(2)]
+        z_plane = [sb.tile([P, S // 2], U8, name=f"z_plane{a}", align_bytes=ALIGN) for a in range(2)]
+        for a in range(2):
+            interleave(nc, z_bf[a][:], z[:, :, halves[a]])
+        for a in range(2):
+            quantize(z_codes[a], z_plane[a], z_bf[a])
 
         olds = sb.tile([P, N // P, S], F32, name="olds", tag=f"diff{PACK - 1}")
-        old = [olds[:, u, :] for u in range(N // P)]
         for u in range(N // P):
-            nc.scalar.activation(old[u], page[u][:].indirect(n3_t[:]), ACT.Copy)
+            nc.scalar.activation(olds[:, u, :], page[u][:].indirect(n3_t[:]), ACT.Copy)
 
-        new = []
-        for u in range(N // P):
-            h_acc = psum.tile([P, S], F32, name=f"h_acc{u}")
+        def layer(u, a, acc):
             nc.tensor.matmul_mx(
-                out=h_acc[:],
+                out=acc,
                 lhsT=w_codes[u][:].bitcast(FP8X4),
                 lhsT_scale=w_plane[u][:],
-                rhs=z_codes[:].bitcast(FP8X4),
-                rhs_scale=z_plane[:],
+                rhs=z_codes[a][:].bitcast(FP8X4),
+                rhs_scale=z_plane[a][:],
                 start=True,
                 stop=True,
             )
-            mix = sb.tile([P, S], F32, name=f"mix{u}")
-            nc.scalar.activation(mix[:], h_acc[:], ACT.Sigmoid)
-            step = sb.tile([P, S], F32, name=f"step{u}")
-            nc.vector.tensor_tensor(step[:], h_acc[:], old[u], ALU.subtract)
-            moved = sb.tile([P, S], F32, name=f"moved{u}")
-            nc.vector.tensor_tensor(moved[:], step[:], mix[:], ALU.mult)
-            fresh = sb.tile([P, S], F32, name=f"fresh{u}")
-            nc.vector.tensor_tensor(fresh[:], moved[:], old[u], ALU.add)
-            new.append(fresh)
+
+        step = [sb.tile([P, S], F32, name=f"step{u}") for u in range(N // P)]
+        mix = [sb.tile([P, S], F32, name=f"mix{u}") for u in range(N // P)]
+        moved = [sb.tile([P, S], F32, name=f"moved{u}") for u in range(N // P)]
+        fresh = [sb.tile([P, S], F32, name=f"fresh{u}") for u in range(N // P)]
+
+        def take_step(u, cols, acc):
+            nc.vector.tensor_tensor(step[u][:, cols], acc, olds[:, u, cols], ALU.subtract)
+
+        def take_mix(u, cols, acc):
+            nc.scalar.activation(mix[u][:, cols], acc, ACT.Sigmoid)
+
+        def blend(u, pieces):
+            for cols in pieces:
+                nc.vector.tensor_tensor(moved[u][:, cols], step[u][:, cols], mix[u][:, cols], ALU.mult)
+            for cols in pieces:
+                nc.vector.tensor_tensor(fresh[u][:, cols], moved[u][:, cols], olds[:, u, cols], ALU.add)
+
+        def whole_block(u):
+            acc = psum.tile([P, S], F32, name=f"h_acc{u}", tag=f"s_acc{u}")
+            for a in range(2):
+                layer(u, a, acc[:, halves[a]])
+            take_mix(u, whole, acc[:])
+            return acc
+
+        whole = slice(0, S)
+        first = [psum.tile([P, S // 2], F32, name=f"h_first{a}") for a in range(2)]
+        for a in range(2):
+            layer(0, a, first[a][:])
+            take_mix(0, halves[a], first[a][:])
+        accs = {1: whole_block(1)}
+        for a in range(2):
+            w_bf[2 + a] = round_weights(2 + a, f"z_bf{a}")
+        for a in range(2):
+            quantize(w_codes[2 + a], w_plane[2 + a], w_bf[2 + a])
+            accs[2 + a] = whole_block(2 + a)
+            take_step(0, halves[a], first[a][:])
+        blend(0, halves)
+        for u in range(1, N // P):
+            take_step(u, whole, accs[u][:])
+            blend(u, [whole])
+
         for u in range(N // P):
-            nc.scalar.activation(page[u][:].indirect(n3_t[:]), new[u][:], ACT.Copy)
+            for cols in halves if u == 0 else [whole]:
+                entries = n3_t[:, cols.start // 16 : cols.stop // 16]
+                nc.scalar.activation(page[u][:].indirect(entries), fresh[u][:, cols], ACT.Copy)
             nc.sync.dma_start(out[P * u : P * (u + 1), :], page[u][:])

@@ -51,9 +51,8 @@ def tile_picked_dwlehqpaget_none_p_kernel(
         d_bytes = sb.tile([P, G], U8, name="d_bytes", tag="d_bytes", align_bytes=ALIGN)
         x_bytes = sb.tile([P, T], U8, name="x_bytes", tag="x_bytes", align_bytes=ALIGN)
 
-        rows = sb.tile([P, 3, 8], F32, name="rows")
 
-        picked_bytes = sb.tile([P, H + S], U8, name="picked_bytes", align_bytes=ALIGN)
+        picked_bytes = sb.tile([P, H + S], U8, name="picked_bytes", tag="picked_bytes", align_bytes=ALIGN)
         planes = sb.tile([P, H + S], U8, name="planes", align_bytes=ALIGN)
         d_codes = sb.tile([P, H], U32, name="d_codes", tag="d_codes", align_bytes=ALIGN)
         x_codes = sb.tile([P, S], U32, name="x_codes", tag="x_codes", align_bytes=ALIGN)
@@ -91,8 +90,9 @@ def tile_picked_dwlehqpaget_none_p_kernel(
 
         w_raw = sb.tile([P, PACK, N], F32, name="w_raw", tag="x_bytes", align_bytes=ALIGN)
         nc.sync.dma_start(w_raw[:], w1.rearrange("(p t) m -> p t m", t=PACK))
+        rows = sb.tile([P, 3, 8], F32, name="rows", tag="picked_bytes", align_bytes=ALIGN)
         for a, vec in enumerate((sl, th, gn)):
-            nc.gpsimd.dma_start(rows[:, a, :PACK], vec.rearrange("(p t) o -> p (t o)", t=PACK))
+            nc.sync.dma_start(rows[:, a, :PACK], vec.rearrange("(p t) o -> p (t o)", t=PACK))
         slope, thresh, gain = rows[:, 0, :PACK], rows[:, 1, :PACK], rows[:, 2, :PACK]
         bias = sb.tile([P, PACK], F32, name="bias")
         slope_thresh = sb.tile([P, PACK], F32, name="slope_thresh")

from contextlib import ExitStack

import concourse.mybir as mybir

K, T, S, N, G, H, U = 512, 2048, 256, 512, 2048, 512, 1024
FLOPS = 2 * K * H * S + 2 * H * N * S

F32 = mybir.dt.float32
BF16 = mybir.dt.bfloat16
I32 = mybir.dt.int32
U32 = mybir.dt.uint32
U16 = mybir.dt.uint16
U8 = mybir.dt.uint8
FP8X4 = mybir.dt.float8_e4m3fn_x4
ACT = mybir.ActivationFunctionType
ALU = mybir.AluOpType

P = 128
PACK = 4
QUADS = 4
QUAD = 32
SPARE = 16
ALIGN = 64
HEAD = 512


def interleave(nc, dst, src):
    nc.vector.tensor_copy(
        out=dst.rearrange("p (c i) t -> p c t i", i=4),
        in_=src.rearrange("p t (c i) -> p c t i", i=4),
    )


def tile_picked_dwlehqpaget_none_p_kernel(
    tc, x_words, x_scales, d_words, d_scales, sl, th, gn, w1, mem, offs, ci, n1, n2, n3, out
):
    nc = tc.nc
    with ExitStack() as ctx:
        lists = ctx.enter_context(tc.tile_pool(name="lists", bufs=1))
        sb = ctx.enter_context(tc.tile_pool(name="sb", bufs=1))
        psum = ctx.enter_context(tc.psum_pool(name="psum", bufs=1))

        ci_t = lists.tile([P, H // 16], U16, name="ci_t")
        offs_t = lists.tile([P, S // 16], U16, name="offs_t")
        n1_t = lists.tile([P, S // 16], U16, name="n1_t")
        n2_t = lists.tile([P, S // 16], U16, name="n2_t")
        n3_t = lists.tile([P, S // 16], U16, name="n3_t")

        d_table = sb.tile([P, G], U32, name="d_table", tag="d_table", align_bytes=ALIGN)
        x_table = sb.tile([P, T], U32, name="x_table", tag="x_table", align_bytes=ALIGN)
        d_bytes = sb.tile([P, G], U8, name="d_bytes", tag="d_bytes", align_bytes=ALIGN)
        x_bytes = sb.tile([P, T], U8, name="x_bytes", tag="x_bytes", align_bytes=ALIGN)


        picked_bytes = sb.tile([P, H + S], U8, name="picked_bytes", tag="picked_bytes", align_bytes=ALIGN)
        planes = sb.tile([P, H + S], U8, name="planes", align_bytes=ALIGN)
        d_codes = sb.tile([P, H], U32, name="d_codes", tag="d_codes", align_bytes=ALIGN)
        x_codes = sb.tile([P, S], U32, name="x_codes", tag="x_codes", align_bytes=ALIGN)
        scores = [sb.tile([P, S + SPARE], F32, name=f"scores{t}") for t in range(PACK)]

        nc.vector.memset(d_bytes[:].bitcast(I32), 0)
        nc.vector.memset(x_bytes[:].bitcast(I32), 0)
        warm = sb.tile([P, 16], F32, name="warm")
        nc.vector.memset(warm[:, :1], 0.0)
        nc.scalar.activation(warm[:, 8:9], warm[:, :1], ACT.Sigmoid)
        nc.vector.memset(planes[:].bitcast(I32), 0)
        for t in range(PACK):
            nc.vector.memset(scores[t][:, S:], 0.0)
        d_src = d_words[0].rearrange("p n t -> p (n t)").bitcast(I32)
        nc.sync.dma_start(d_table[:, :HEAD].bitcast(I32), d_src[:, :HEAD])
        nc.sync.dma_start(ci_t[:], ci)
        nc.sync.dma_start(d_bytes[0:P:8, :].bitcast(I32), d_scales[0].bitcast(I32))
        nc.sync.dma_start(offs_t[:], offs)
        nc.sync.dma_start(x_bytes[0:P:8, :].bitcast(I32), x_scales[0].bitcast(I32))
        nc.sync.dma_start(d_table[:, HEAD:].bitcast(I32), d_src[:, HEAD:])
        nc.sync.dma_start(n1_t[:], n1)
        nc.sync.dma_start(x_table[:].bitcast(I32), x_words[0].rearrange("p n t -> p (n t)").bitcast(I32))
        nc.sync.dma_start(n2_t[:], n2)
        nc.sync.dma_start(n3_t[:], n3)

        nc.vector.tensor_copy(picked_bytes[:, :H].rearrange("p (t m) -> p m t", t=PACK), d_bytes[:].indirect(ci_t[:]))
        nc.vector.tensor_copy(picked_bytes[:, H:], x_bytes[:].indirect(offs_t[:]))
        for q in range(QUADS):
            nc.sync.dma_start(
                planes[QUAD * q : QUAD * q + 4, :].bitcast(I32), picked_bytes[QUAD * q : QUAD * (q + 1) : 8, :].bitcast(I32)
            )
        d_plane, x_plane = planes[:, :H], planes[:, H:]
        nc.vector.tensor_copy(d_codes[:].rearrange("p (t m) -> p m t", t=PACK), d_table[:].indirect(ci_t[:]))
        nc.vector.tensor_copy(x_codes[:], x_table[:].indirect(offs_t[:]))

        w_raw = sb.tile([P, PACK, N], F32, name="w_raw", tag="x_bytes", align_bytes=ALIGN)
        nc.sync.dma_start(w_raw[:], w1.rearrange("(p t) m -> p t m", t=PACK))
        rows = sb.tile([P, 3, 8], F32, name="rows", tag="picked_bytes", align_bytes=ALIGN)
        for a, vec in enumerate((sl, th, gn)):
            nc.sync.dma_start(rows[:, a, :PACK], vec.rearrange("(p t) o -> p (t o)", t=PACK))
        slope, thresh, gain = rows[:, 0, :PACK], rows[:, 1, :PACK], rows[:, 2, :PACK]
        bias = sb.tile([P, PACK], F32, name="bias")
        slope_thresh = sb.tile([P, PACK], F32, name="slope_thresh")
        nc.gpsimd.tensor_tensor(slope_thresh[:], slope, thresh, ALU.mult)
        nc.gpsimd.tensor_scalar(bias[:], slope_thresh[:], -1.0, None, ALU.mult)

        s_acc = [psum.tile([P, S], F32, name=f"s_acc{t}", tag=f"s_acc{t}") for t in range(PACK)]
        for t in range(PACK):
            cols = slice(P * t, P * (t + 1))
            nc.tensor.matmul_mx(
                out=s_acc[t][:],
                lhsT=d_codes[:, cols].bitcast(FP8X4),
                lhsT_scale=d_plane[:, cols],
                rhs=x_codes[:].bitcast(FP8X4),
                rhs_scale=x_plane,
                start=True,
                stop=True,
            )

        page_tags = ("d_table", "x_table", "d_codes", "x_codes")
        page = [sb.tile([P, U], F32, name=f"page{u}", tag=page_tags[u], align_bytes=ALIGN) for u in range(N // P)]
        for u in range(N // P):
            nc.sync.dma_start(page[u][:], mem[P * u : P * (u + 1), :])

        w_codes = [sb.tile([P, P], U32, name=f"w_codes{u}", align_bytes=ALIGN) for u in range(N // P)]
        w_plane = [sb.tile([P, P], U8, name=f"w_plane{u}", align_bytes=ALIGN) for u in range(N // P)]

        def quantize(codes, plane, grouped):
            nc.vector.quantize_mx(
                out=codes[:].bitcast(FP8X4), scales=plane[:], in_=grouped[:].rearrange("p c t -> p (c t)")
            )

        def round_weights(u, tag):
            grouped = sb.tile([P, P, PACK], BF16, name=f"w_bf{u}", tag=tag, align_bytes=ALIGN)
            interleave(nc, grouped[:], w_raw[:, :, P * u : P * (u + 1)])
            return grouped

        for t in range(PACK):
            nc.vector.tensor_scalar(scores[t][:, :S], s_acc[t][:], 0.0625, None, ALU.mult)
        diff = [sb.tile([P, 2 * S], F32, name=f"diff{t}", tag=f"diff{t}") for t in range(PACK)]
        w_bf = {}
        for t in range(PACK):
            nc.scalar.activation(diff[t][:, S:], scores[t][:].indirect(n1_t[:]), ACT.Copy)
            nc.vector.tensor_tensor(diff[t][:, :S], scores[t][:, :S], diff[t][:, S:], ALU.subtract)
            if t % 2 == 1:
                w_bf[t // 2] = round_weights(t // 2, f"w_bf{t // 2}")

        z = sb.tile([P, PACK, S], F32, name="z", tag="z", align_bytes=ALIGN)
        for t in range(PACK):
            gate = sb.tile([P, S], F32, name=f"gate{t}")
            nc.scalar.activation(
                gate[:],
                diff[t][:].indirect(n2_t[:]),
                ACT.Sigmoid,
                bias=bias[:, t : t + 1],
                scale=slope[:, t : t + 1],
            )
            nc.vector.scalar_tensor_tensor(
                z[:, t, :], scores[t][:, :S], gain[:, t : t + 1], gate[:], ALU.mult, ALU.mult
            )
            if t < 2:
                quantize(w_codes[t], w_plane[t], w_bf[t])
        halves = [slice(0, S // 2), slice(S // 2, S)]
        z_bf = [sb.tile([P, S // 2, PACK], BF16, name=f"z_bf{a}", tag=f"z_bf{a}", align_bytes=ALIGN) for a in range(2)]
        z_codes = [sb.tile([P, S // 2], U32, name=f"z_codes{a}", align_bytes=ALIGN) for a in range(2)]
        z_plane = [sb.tile([P, S // 2], U8, name=f"z_plane{a}", align_bytes=ALIGN) for a in range(2)]
        for a in range(2):
            interleave(nc, z_bf[a][:], z[:, :, halves[a]])
        for a in range(2):
            quantize(z_codes[a], z_plane[a], z_bf[a])

        olds = sb.tile([P, N // P, S], F32, name="olds", tag=f"diff{PACK - 1}")
        for u in range(N // P):
            nc.scalar.activation(olds[:, u, :], page[u][:].indirect(n3_t[:]), ACT.Copy)

        def layer(u, a, acc):
            nc.tensor.matmul_mx(
                out=acc,
                lhsT=w_codes[u][:].bitcast(FP8X4),
                lhsT_scale=w_plane[u][:],
                rhs=z_codes[a][:].bitcast(FP8X4),
                rhs_scale=z_plane[a][:],
                start=True,
                stop=True,
            )

        step = [sb.tile([P, S], F32, name=f"step{u}") for u in range(N // P)]
        mix = [sb.tile([P, S], F32, name=f"mix{u}") for u in range(N // P)]
        moved = [sb.tile([P, S], F32, name=f"moved{u}") for u in range(N // P)]
        fresh = [sb.tile([P, S], F32, name=f"fresh{u}") for u in range(N // P)]

        def take_step(u, cols, acc):
            nc.vector.tensor_tensor(step[u][:, cols], acc, olds[:, u, cols], ALU.subtract)

        def take_mix(u, cols, acc):
            nc.scalar.activation(mix[u][:, cols], acc, ACT.Sigmoid)

        def blend(u, pieces):
            for cols in pieces:
                nc.vector.tensor_tensor(moved[u][:, cols], step[u][:, cols], mix[u][:, cols], ALU.mult)
            for cols in pieces:
                nc.vector.tensor_tensor(fresh[u][:, cols], moved[u][:, cols], olds[:, u, cols], ALU.add)

        def whole_block(u):
            acc = psum.tile([P, S], F32, name=f"h_acc{u}", tag=f"s_acc{u}")
            for a in range(2):
                layer(u, a, acc[:, halves[a]])
            take_mix(u, whole, acc[:])
            return acc

        whole = slice(0, S)
        first = [psum.tile([P, S // 2], F32, name=f"h_first{a}") for a in range(2)]
        for a in range(2):
            layer(0, a, first[a][:])
            take_mix(0, halves[a], first[a][:])
        accs = {1: whole_block(1)}
        for a in range(2):
            w_bf[2 + a] = round_weights(2 + a, f"z_bf{a}")
        for a in range(2):
            quantize(w_codes[2 + a], w_plane[2 + a], w_bf[2 + a])
            accs[2 + a] = whole_block(2 + a)
            take_step(0, halves[a], first[a][:])
        blend(0, halves)
        for u in range(1, N // P):
            take_step(u, whole, accs[u][:])
            blend(u, [whole])

        for u in range(N // P):
            for cols in halves if u == 0 else [whole]:
                entries = n3_t[:, cols.start // 16 : cols.stop // 16]
                nc.scalar.activation(page[u][:].indirect(entries), fresh[u][:, cols], ACT.Copy)
            nc.sync.dma_start(out[P * u : P * (u + 1), :], page[u][:])
